import numpy as np
import ml_dtypes


def mxq(x, axis, fmt="e4m3"):
    dtype, down = {"e4m3": (ml_dtypes.float8_e4m3fn, 7), "e5m2": (ml_dtypes.float8_e5m2, 14)}[fmt]
    v = np.moveaxis(np.asarray(x, np.float32).astype(ml_dtypes.bfloat16).astype(np.float64), axis, -1)
    blocks = v.reshape(v.shape[:-1] + (-1, 32))
    amax = np.abs(blocks).max(-1, keepdims=True)
    byte = np.maximum(np.where(amax > 0, np.frexp(amax)[1] - 1 + 127, 0) - down, 1)
    scale = np.exp2(byte - 127.0)
    codes = (blocks / scale).astype(np.float32).astype(dtype).astype(np.float64)
    return np.moveaxis((codes * scale).reshape(v.shape), -1, axis)


WIDE = False


def mx_kscale(k):
    if not WIDE:
        return np.ones(k)
    levels = np.array([30, -30])
    if k % 512:
        return np.exp2(np.random.permutation(np.resize(levels, k // 32))).repeat(32)
    a = np.empty((k // 512, 16))
    for p in range(k // 512):
        a[p, :8] = np.random.permutation(np.resize(levels, 8))
        for g in range(8):
            far = levels[np.abs(levels - a[p, g]) >= 10]
            a[p, g + 8] = far[np.random.randint(len(far))]
    return np.exp2(a.ravel()).repeat(32)


def f64(x):
    return np.asarray(x).astype(np.float64)


def striped(idx):
    return np.tile(np.asarray(idx).reshape(-1, 16).T, (8, 1)).astype(np.uint16)


def unstriped(offs):
    return offs[:16].T.reshape(-1).astype(np.int64)


E2M1 = np.array([0.0, 0.5, 1.0, 1.5, 2.0, 3.0, 4.0, 6.0, -0.0, -0.5, -1.0, -1.5, -2.0, -3.0, -4.0, -6.0])


def pack_weight(w, fmt):
    k, n = w.shape
    w = f64(np.asarray(w, np.float32).astype(ml_dtypes.bfloat16)).reshape(k // 32, 32, n)
    amax = np.abs(w).max(1)
    if fmt in ("e4m3", "e5m2"):
        byte = np.frexp(amax)[1] - 1 + 127 - (7 if fmt == "e4m3" else 14)
    else:
        mant, ex = np.frexp(amax / 6.0)
        byte = np.where(mant > 0.5, ex, ex - 1) + 127
    byte = np.clip(np.where(amax > 0, byte, 1), 1, 254)
    scaled = (w * np.exp2(127.0 - byte)[:, None, :]).reshape(k, n).astype(np.float32)
    by_word = np.ascontiguousarray(scaled.reshape(k // 512, 128, 4, n).transpose(0, 1, 3, 2))
    if fmt in ("e4m3", "e5m2"):
        words = by_word.astype(ml_dtypes.float8_e4m3fn if fmt == "e4m3" else ml_dtypes.float8_e5m2).view(np.uint8)
    else:
        c = by_word.astype(ml_dtypes.float4_e2m1fn).view(np.uint8) & 0xF
        words = (c[..., 0::2] | (c[..., 1::2] << 4)).reshape(k // 512, 128, 2 * n)
    return np.ascontiguousarray(words), np.ascontiguousarray(byte.astype(np.uint8).reshape(k // 512, 16, n))


def unpack_weight(words, scales, fmt):
    g, _, n = scales.shape
    words = np.ascontiguousarray(words).reshape(g, 128, n, -1)
    if fmt in ("e4m3", "e5m2"):
        vals = words.view(ml_dtypes.float8_e4m3fn if fmt == "e4m3" else ml_dtypes.float8_e5m2).astype(np.float64)
    else:
        nib = np.empty((g, 128, n, 4), np.uint8)
        nib[..., 0::2] = words & 0xF
        nib[..., 1::2] = words >> 4
        vals = E2M1[nib]
    vals = vals * np.repeat(np.exp2(scales.astype(np.float64) - 127.0), 8, axis=1)[..., None]
    return vals.transpose(0, 1, 3, 2).reshape(g * 512, n)


K, T, J, I, R, E = 512, 512, 256, 256, 512, 32


def setup_inputs():
    n = np.random.standard_normal
    idx = np.random.permutation(T)[:J]
    idx2 = np.random.permutation(T)[:I]
    fk = mx_kscale(K)
    fr = mx_kscale(R)
    xtp = pack_weight(n((K, T)) / fk[:, None], "e2m1")
    wap = pack_weight(n((K, R)) * 0.5 / np.sqrt(K) * fk[:, None] * fr, "e2m1")
    wbp = pack_weight(n((K, R)) * 1 / np.sqrt(K) * fk[:, None] / fr, "e5m2")
    return {
        "xt_words": xtp[0],
        "xt_scales": xtp[1],
        "wa_words": wap[0],
        "wa_scales": wap[1],
        "wb_words": wbp[0],
        "wb_scales": wbp[1],
        "offs": striped(idx),
        "offs2": striped(idx2),
    }


def reference(xt_words, xt_scales, wa_words, wa_scales, wb_words, wb_scales, offs, offs2):
    idx = unstriped(offs)
    idx2 = unstriped(offs2)
    xtu = unpack_weight(xt_words, xt_scales, "e2m1")
    wau = unpack_weight(wa_words, wa_scales, "e2m1")
    wbu = unpack_weight(wb_words, wb_scales, "e5m2")
    xtidxg = xtu[:, idx]
    za = wau.T @ xtidxg
    ma1 = za.reshape(R, E, J // E).mean(axis=2)
    ma2 = np.repeat(ma1, J // E, axis=1)
    ha = za - ma2
    xtidx2g = xtu[:, idx2]
    zb = wbu.T @ xtidx2g
    yb1 = np.pad(zb, ((0, 0), (1, 0)))[:, :I]
    hb = zb - 0.6 * yb1
    haq = mxq(ha, 0, "e5m2")
    hbq = mxq(hb, 0, "e4m3")
    a0 = haq.T @ hbq
    a1 = np.pad(a0, ((0, 0), (1, 0)))[:, :I]
    y = 0.04 * np.abs(a0 - a1)
    return y

@@ -1,0 +1,218 @@
+from contextlib import ExitStack
+
+import concourse.mybir as mybir
+
+K, T, J, I, R = 512, 512, 256, 256, 512
+FLOPS = 2 * K * R * J + 2 * K * R * I + 2 * R * J * I
+
+F32 = mybir.dt.float32
+BF16 = mybir.dt.bfloat16
+I32 = mybir.dt.int32
+U32 = mybir.dt.uint32
+U16 = mybir.dt.uint16
+U8 = mybir.dt.uint8
+E2M1 = mybir.dt.float4_e2m1fn_x4
+E5M2 = mybir.dt.float8_e5m2_x4
+E4M3 = mybir.dt.float8_e4m3fn_x4
+ALU = mybir.AluOpType
+ACT = mybir.ActivationFunctionType
+
+P = 128
+PACK = 4
+HALF = 128
+BUNDLE = 8
+LAG = 0.6
+GAIN = 0.04
+
+
+def load_scale_rows(queue, plane, scales):
+    rows = scales[0].bitcast(I32)
+    for q in range(4):
+        queue.dma_start(out=plane[32 * q : 32 * q + 4, :].bitcast(I32), in_=rows[4 * q : 4 * q + 4, :])
+
+
+def deal_columns(nc, dealt, loaded):
+    nc.scalar.copy(
+        out=dealt[:].bitcast(U32).rearrange("p (t g w) -> p t g w", t=PACK, g=16),
+        in_=loaded[:].bitcast(U32).rearrange("p (g t w) -> p t g w", t=PACK, g=16),
+    )
+
+
+def tile_list_meet_levelled_lagged_steps_kernel(
+    tc, xt_words, xt_scales, wa_words, wa_scales, wb_words, wb_scales, offs, offs2, out
+):
+    nc = tc.nc
+    with ExitStack() as ctx:
+        sb = ctx.enter_context(tc.tile_pool(name="sb", bufs=1))
+        ps = ctx.enter_context(tc.psum_pool(name="ps", bufs=1))
+
+        list_a = sb.tile([P, J // 16], U16, name="list_a")
+        list_b = sb.tile([P, I // 16], U16, name="list_b")
+        x_words = sb.tile([P, T], U16, name="x_words", align_bytes=64)
+        x_plane = sb.tile([P, T], U8, name="x_plane", align_bytes=64)
+        wa_in = sb.tile([P, 2 * R], U8, name="wa_in", align_bytes=64)
+        wb_in = sb.tile([P, 4 * R], U8, name="wb_in", align_bytes=64)
+        wa_plane_in = sb.tile([P, R], U8, name="wa_plane_in", align_bytes=64)
+        wb_plane_in = sb.tile([P, R], U8, name="wb_plane_in", align_bytes=64)
+        wa = sb.tile([P, 2 * R], U8, name="wa", align_bytes=64)
+        wb = sb.tile([P, 4 * R], U8, name="wb", align_bytes=64)
+        wa_plane = sb.tile([P, R], U8, name="wa_plane", align_bytes=64)
+        wb_plane = sb.tile([P, R], U8, name="wb_plane", align_bytes=64)
+        xa_words = sb.tile([P, J], U16, name="xa_words", align_bytes=64)
+        xa_plane = sb.tile([P, J], U8, name="xa_plane", align_bytes=64)
+        xb_words = sb.tile([P, I], U16, name="xb_words", align_bytes=64)
+        xb_plane = sb.tile([P, I], U8, name="xb_plane", align_bytes=64)
+        lagged = sb.tile([P, PACK * (I + 1)], F32, name="lagged", align_bytes=64)
+        before = [sb.tile([P, I + 4], F32, name=f"before{a}", align_bytes=64) for a in range(2)]
+
+        nc.gpsimd.memset(x_plane[:].bitcast(I32), 0)
+        nc.gpsimd.memset(wa_plane_in[:].bitcast(I32), 0)
+        nc.gpsimd.memset(wb_plane_in[:].bitcast(I32), 0)
+        nc.gpsimd.memset(lagged[:, 0:PACK], 0.0)
+        for a in range(2):
+            nc.gpsimd.memset(before[a][:, 3:4], 0.0)
+
+        nc.sync.dma_start(list_a[:], offs)
+        nc.scalar.dma_start(out=x_words[:].bitcast(I32), in_=xt_words[0].bitcast(I32))
+        load_scale_rows(nc.sync, x_plane, xt_scales)
+        nc.sync.dma_start(list_b[:], offs2)
+        nc.scalar.dma_start(out=wa_in[:].bitcast(I32), in_=wa_words[0].bitcast(I32))
+        load_scale_rows(nc.sync, wa_plane_in, wa_scales)
+        nc.sync.dma_start(out=wb_in[:].bitcast(I32), in_=wb_words[0].rearrange("p n t -> p (n t)").bitcast(I32))
+        load_scale_rows(nc.sync, wb_plane_in, wb_scales)
+
+        nc.vector.tensor_copy(xa_words[:], x_words[:].indirect(list_a[:]))
+        nc.vector.tensor_copy(xa_plane[:], x_plane[:].indirect(list_a[:]))
+        nc.vector.tensor_copy(xb_words[:], x_words[:].indirect(list_b[:]))
+        nc.vector.tensor_copy(xb_plane[:], x_plane[:].indirect(list_b[:]))
+
+        deal_columns(nc, wa, wa_in)
+        deal_columns(nc, wa_plane, wa_plane_in)
+        deal_columns(nc, wb, wb_in)
+        deal_columns(nc, wb_plane, wb_plane_in)
+
+        za = [ps.tile([P, PACK, HALF], F32, name=f"za{h}") for h in range(2)]
+        zb = [ps.tile([P, PACK, HALF], F32, name=f"zb{h}") for h in range(2)]
+        scores = [[ps.tile([P, HALF], F32, name=f"scores{h}{a}") for a in range(2)] for h in range(2)]
+
+        for h in range(2):
+            cols = slice(h * HALF, (h + 1) * HALF)
+            for t in range(PACK):
+                nc.tensor.matmul_mx(
+                    out=za[h][:, t, :],
+                    lhsT=wa[:, 2 * P * t : 2 * P * (t + 1)].bitcast(E2M1),
+                    lhsT_scale=wa_plane[:, P * t : P * (t + 1)],
+                    rhs=xa_words[:, cols].bitcast(E2M1),
+                    rhs_scale=xa_plane[:, cols],
+                    start=True,
+                    stop=True,
+                )
+        for h in range(2):
+            cols = slice(h * HALF, (h + 1) * HALF)
+            for t in range(PACK):
+                nc.tensor.matmul_mx(
+                    out=zb[h][:, t, :],
+                    lhsT=wb[:, 4 * P * t : 4 * P * (t + 1)].bitcast(E5M2),
+                    lhsT_scale=wb_plane[:, P * t : P * (t + 1)],
+                    rhs=xb_words[:, cols].bitcast(E2M1),
+                    rhs_scale=xb_plane[:, cols],
+                    start=True,
+                    stop=True,
+                )
+
+        bundles = HALF // BUNDLE
+        sums = [sb.tile([P, PACK, bundles], F32, name=f"sums{h}", align_bytes=64) for h in range(2)]
+        means = [sb.tile([P, bundles, PACK], F32, name=f"means{h}", align_bytes=64) for h in range(2)]
+        ha = sb.tile([P, J * PACK], BF16, name="ha", align_bytes=64)
+        ha_codes = sb.tile([P, J], U32, name="ha_codes", align_bytes=64)
+        ha_plane = sb.tile([P, J], U8, name="ha_plane", align_bytes=64)
+        for h in range(2):
+            nc.vector.tensor_reduce(
+                out=sums[h][:],
+                in_=za[h][:].rearrange("p t (e u) -> p t e u", u=BUNDLE),
+                axis=mybir.AxisListType.X,
+                op=ALU.add,
+            )
+            nc.gpsimd.tensor_scalar(
+                out=means[h][:],
+                in0=sums[h][:].rearrange("p t e -> p e t"),
+                scalar1=1.0 / BUNDLE,
+                scalar2=0.0,
+                op0=ALU.mult,
+                op1=ALU.add,
+            )
+        for h in range(2):
+            nc.vector.tensor_tensor(
+                out=ha[:, h * HALF * PACK : (h + 1) * HALF * PACK].rearrange("p (e u t) -> p e u t", u=BUNDLE, t=PACK),
+                in0=za[h][:].rearrange("p t (e u) -> p e u t", u=BUNDLE),
+                in1=means[h][:].unsqueeze(2).broadcast_to([P, bundles, BUNDLE, PACK]),
+                op=ALU.subtract,
+            )
+
+        hb = [sb.tile([P, HALF * PACK], BF16, name=f"hb{h}", align_bytes=64) for h in range(2)]
+        hb_codes = [sb.tile([P, HALF], U32, name=f"hb_codes{h}", align_bytes=64) for h in range(2)]
+        hb_plane = [sb.tile([P, HALF], U8, name=f"hb_plane{h}", align_bytes=64) for h in range(2)]
+        steps = [sb.tile([P, 2, HALF], F32, name=f"steps{h}", align_bytes=64) for h in range(2)]
+        result = [sb.tile([P, 2, HALF], F32, name=f"result{h}", align_bytes=64) for h in range(2)]
+
+        def lag(h):
+            start = PACK * (h * HALF + 1)
+            nc.scalar.activation(
+                out=lagged[:, start : start + PACK * HALF].rearrange("p (i t) -> p i t", t=PACK),
+                in_=zb[h][:].rearrange("p t i -> p i t"),
+                func=ACT.Copy,
+                scale=-LAG,
+            )
+
+        def make_hb(h):
+            start = PACK * h * HALF
+            nc.vector.tensor_tensor(
+                out=hb[h][:].rearrange("p (i t) -> p i t", t=PACK),
+                in0=zb[h][:].rearrange("p t i -> p i t"),
+                in1=lagged[:, start : start + PACK * HALF].rearrange("p (i t) -> p i t", t=PACK),
+                op=ALU.add,
+            )
+
+        def quantize_hb(h):
+            nc.vector.quantize_mx(out=hb_codes[h][:].bitcast(E4M3), scales=hb_plane[h][:], in_=hb[h][:])
+
+        def meet(h):
+            for a in range(2):
+                rows = slice(a * P, (a + 1) * P)
+                nc.tensor.matmul_mx(
+                    out=scores[h][a][:],
+                    lhsT=ha_codes[:, rows].bitcast(E5M2),
+                    lhsT_scale=ha_plane[:, rows],
+                    rhs=hb_codes[h][:].bitcast(E4M3),
+                    rhs_scale=hb_plane[h][:],
+                    start=True,
+                    stop=True,
+                )
+            for a in range(2):
+                nc.scalar.copy(out=before[a][:, 4 + h * HALF : 4 + (h + 1) * HALF], in_=scores[h][a][:])
+
+        def finish(h):
+            for a in range(2):
+                nc.vector.tensor_tensor(
+                    out=steps[h][:, a, :],
+                    in0=scores[h][a][:],
+                    in1=before[a][:, 3 + h * HALF : 3 + (h + 1) * HALF],
+                    op=ALU.subtract,
+                )
+            for a in range(2):
+                nc.scalar.activation(out=result[h][:, a, :], in_=steps[h][:, a, :], func=ACT.Abs, scale=GAIN)
+            nc.sync.dma_start(
+                out=out[:, h * HALF : (h + 1) * HALF].rearrange("(a p) i -> p a i", p=P), in_=result[h][:]
+            )
+
+        lag(0)
+        lag(1)
+        make_hb(0)
+        nc.vector.quantize_mx(out=ha_codes[:].bitcast(E5M2), scales=ha_plane[:], in_=ha[:])
+        quantize_hb(0)
+        make_hb(1)
+        meet(0)
+        quantize_hb(1)
+        meet(1)
+        finish(0)
+        finish(1)

@@ -25,10 +25,19 @@ LAG = 0.6
 GAIN = 0.04
 
 
-def load_scale_rows(queue, plane, scales):
+def load_scale_rows(queues, plane, scales):
+    rows = scales[0].bitcast(I32)
+    for q, queue in enumerate(queues):
+        queue.dma_start(out=plane[32 * q : 32 * q + 4, :].bitcast(I32), in_=rows[4 * q : 4 * q + 4, :])
+
+
+def load_scale_rows_repeated(queue, plane, scales):
     rows = scales[0].bitcast(I32)
     for q in range(4):
-        queue.dma_start(out=plane[32 * q : 32 * q + 4, :].bitcast(I32), in_=rows[4 * q : 4 * q + 4, :])
+        queue.dma_start(
+            out=plane[32 * q : 32 * (q + 1), :].bitcast(I32),
+            in_=rows[4 * q : 4 * q + 4, :].partition_broadcast(8),
+        )
 
 
 def deal_columns(nc, dealt, loaded):
@@ -65,7 +74,6 @@ def tile_list_meet_levelled_lagged_steps_kernel(
         lagged = sb.tile([P, PACK * (I + 1)], F32, name="lagged", align_bytes=64)
         before = [sb.tile([P, I + 4], F32, name=f"before{a}", align_bytes=64) for a in range(2)]
 
-        nc.gpsimd.memset(x_plane[:].bitcast(I32), 0)
         nc.gpsimd.memset(wa_plane_in[:].bitcast(I32), 0)
         nc.gpsimd.memset(wb_plane_in[:].bitcast(I32), 0)
         nc.gpsimd.memset(lagged[:, 0:PACK], 0.0)
@@ -74,12 +82,12 @@ def tile_list_meet_levelled_lagged_steps_kernel(
 
         nc.sync.dma_start(list_a[:], offs)
         nc.scalar.dma_start(out=x_words[:].bitcast(I32), in_=xt_words[0].bitcast(I32))
-        load_scale_rows(nc.sync, x_plane, xt_scales)
         nc.sync.dma_start(list_b[:], offs2)
         nc.scalar.dma_start(out=wa_in[:].bitcast(I32), in_=wa_words[0].bitcast(I32))
-        load_scale_rows(nc.sync, wa_plane_in, wa_scales)
+        load_scale_rows_repeated(nc.sync, x_plane, xt_scales)
+        load_scale_rows([nc.sync] * 4, wa_plane_in, wa_scales)
         nc.sync.dma_start(out=wb_in[:].bitcast(I32), in_=wb_words[0].rearrange("p n t -> p (n t)").bitcast(I32))
-        load_scale_rows(nc.sync, wb_plane_in, wb_scales)
+        load_scale_rows([nc.gpsimd] + [nc.sync] * 3, wb_plane_in, wb_scales)
 
         nc.vector.tensor_copy(xa_words[:], x_words[:].indirect(list_a[:]))
         nc.vector.tensor_copy(xa_plane[:], x_plane[:].indirect(list_a[:]))
@@ -121,7 +129,7 @@ def tile_list_meet_levelled_lagged_steps_kernel(
                 )
 
         bundles = HALF // BUNDLE
-        sums = [sb.tile([P, PACK, bundles], F32, name=f"sums{h}", align_bytes=64) for h in range(2)]
+        sums = [sb.tile([P, bundles, PACK], F32, name=f"sums{h}", align_bytes=64) for h in range(2)]
         means = [sb.tile([P, bundles, PACK], F32, name=f"means{h}", align_bytes=64) for h in range(2)]
         ha = sb.tile([P, J * PACK], BF16, name="ha", align_bytes=64)
         ha_codes = sb.tile([P, J], U32, name="ha_codes", align_bytes=64)
@@ -129,13 +137,13 @@ def tile_list_meet_levelled_lagged_steps_kernel(
         for h in range(2):
             nc.vector.tensor_reduce(
                 out=sums[h][:],
-                in_=za[h][:].rearrange("p t (e u) -> p t e u", u=BUNDLE),
+                in_=za[h][:].rearrange("p t (e u) -> p e t u", u=BUNDLE),
                 axis=mybir.AxisListType.X,
                 op=ALU.add,
             )
             nc.gpsimd.tensor_scalar(
                 out=means[h][:],
-                in0=sums[h][:].rearrange("p t e -> p e t"),
+                in0=sums[h][:],
                 scalar1=1.0 / BUNDLE,
                 scalar2=0.0,
                 op0=ALU.mult,
@@ -153,7 +161,7 @@ def tile_list_meet_levelled_lagged_steps_kernel(
         hb_codes = [sb.tile([P, HALF], U32, name=f"hb_codes{h}", align_bytes=64) for h in range(2)]
         hb_plane = [sb.tile([P, HALF], U8, name=f"hb_plane{h}", align_bytes=64) for h in range(2)]
         steps = [sb.tile([P, 2, HALF], F32, name=f"steps{h}", align_bytes=64) for h in range(2)]
-        result = [sb.tile([P, 2, HALF], F32, name=f"result{h}", align_bytes=64) for h in range(2)]
+        result = [[sb.tile([P, HALF], F32, name=f"result{h}{a}", align_bytes=64) for a in range(2)] for h in range(2)]
 
         def lag(h):
             start = PACK * (h * HALF + 1)
@@ -199,11 +207,9 @@ def tile_list_meet_levelled_lagged_steps_kernel(
                     in1=before[a][:, 3 + h * HALF : 3 + (h + 1) * HALF],
                     op=ALU.subtract,
                 )
-            for a in range(2):
-                nc.scalar.activation(out=result[h][:, a, :], in_=steps[h][:, a, :], func=ACT.Abs, scale=GAIN)
-            nc.sync.dma_start(
-                out=out[:, h * HALF : (h + 1) * HALF].rearrange("(a p) i -> p a i", p=P), in_=result[h][:]
-            )
+            for a, queue in enumerate((nc.sync, nc.scalar)):
+                nc.scalar.activation(out=result[h][a][:], in_=steps[h][:, a, :], func=ACT.Abs, scale=GAIN)
+                queue.dma_start(out=out[a * P : (a + 1) * P, h * HALF : (h + 1) * HALF], in_=result[h][a][:])
 
         lag(0)
         lag(1)

@@ -31,9 +31,9 @@ def load_scale_rows(queues, plane, scales):
         queue.dma_start(out=plane[32 * q : 32 * q + 4, :].bitcast(I32), in_=rows[4 * q : 4 * q + 4, :])
 
 
-def load_scale_rows_repeated(queue, plane, scales):
+def load_scale_rows_repeated(queues, plane, scales):
     rows = scales[0].bitcast(I32)
-    for q in range(4):
+    for q, queue in enumerate(queues):
         queue.dma_start(
             out=plane[32 * q : 32 * (q + 1), :].bitcast(I32),
             in_=rows[4 * q : 4 * q + 4, :].partition_broadcast(8),
@@ -82,9 +82,9 @@ def tile_list_meet_levelled_lagged_steps_kernel(
 
         nc.sync.dma_start(list_a[:], offs)
         nc.scalar.dma_start(out=x_words[:].bitcast(I32), in_=xt_words[0].bitcast(I32))
+        load_scale_rows_repeated([nc.sync, nc.scalar, nc.sync, nc.scalar], x_plane, xt_scales)
         nc.sync.dma_start(list_b[:], offs2)
-        nc.scalar.dma_start(out=wa_in[:].bitcast(I32), in_=wa_words[0].bitcast(I32))
-        load_scale_rows_repeated(nc.sync, x_plane, xt_scales)
+        nc.sync.dma_start(out=wa_in[:].bitcast(I32), in_=wa_words[0].bitcast(I32))
         load_scale_rows([nc.sync] * 4, wa_plane_in, wa_scales)
         nc.sync.dma_start(out=wb_in[:].bitcast(I32), in_=wb_words[0].rearrange("p n t -> p (n t)").bitcast(I32))
         load_scale_rows([nc.gpsimd] + [nc.sync] * 3, wb_plane_in, wb_scales)

from contextlib import ExitStack

import concourse.mybir as mybir

K, T, J, I, R = 512, 512, 256, 256, 512
FLOPS = 2 * K * R * J + 2 * K * R * I + 2 * R * J * I

F32 = mybir.dt.float32
BF16 = mybir.dt.bfloat16
I32 = mybir.dt.int32
U32 = mybir.dt.uint32
U16 = mybir.dt.uint16
U8 = mybir.dt.uint8
E2M1 = mybir.dt.float4_e2m1fn_x4
E5M2 = mybir.dt.float8_e5m2_x4
E4M3 = mybir.dt.float8_e4m3fn_x4
ALU = mybir.AluOpType
ACT = mybir.ActivationFunctionType

P = 128
PACK = 4
HALF = 128
BUNDLE = 8
LAG = 0.6
GAIN = 0.04


def load_scale_rows(queues, plane, scales):
    rows = scales[0].bitcast(I32)
    for q, queue in enumerate(queues):
        queue.dma_start(out=plane[32 * q : 32 * q + 4, :].bitcast(I32), in_=rows[4 * q : 4 * q + 4, :])


def load_scale_rows_repeated(queues, plane, scales):
    rows = scales[0].bitcast(I32)
    for q, queue in enumerate(queues):
        queue.dma_start(
            out=plane[32 * q : 32 * (q + 1), :].bitcast(I32),
            in_=rows[4 * q : 4 * q + 4, :].partition_broadcast(8),
        )


def deal_columns(nc, dealt, loaded):
    nc.scalar.copy(
        out=dealt[:].bitcast(U32).rearrange("p (t g w) -> p t g w", t=PACK, g=16),
        in_=loaded[:].bitcast(U32).rearrange("p (g t w) -> p t g w", t=PACK, g=16),
    )


def tile_list_meet_levelled_lagged_steps_kernel(
    tc, xt_words, xt_scales, wa_words, wa_scales, wb_words, wb_scales, offs, offs2, out
):
    nc = tc.nc
    with ExitStack() as ctx:
        sb = ctx.enter_context(tc.tile_pool(name="sb", bufs=1))
        ps = ctx.enter_context(tc.psum_pool(name="ps", bufs=1))

        list_a = sb.tile([P, J // 16], U16, name="list_a")
        list_b = sb.tile([P, I // 16], U16, name="list_b")
        x_words = sb.tile([P, T], U16, name="x_words", align_bytes=64)
        x_plane = sb.tile([P, T], U8, name="x_plane", align_bytes=64)
        wa_in = sb.tile([P, 2 * R], U8, name="wa_in", align_bytes=64)
        wb_in = sb.tile([P, 4 * R], U8, name="wb_in", align_bytes=64)
        wa_plane_in = sb.tile([P, R], U8, name="wa_plane_in", align_bytes=64)
        wb_plane_in = sb.tile([P, R], U8, name="wb_plane_in", align_bytes=64)
        wa = sb.tile([P, 2 * R], U8, name="wa", align_bytes=64)
        wb = sb.tile([P, 4 * R], U8, name="wb", align_bytes=64)
        wa_plane = sb.tile([P, R], U8, name="wa_plane", align_bytes=64)
        wb_plane = sb.tile([P, R], U8, name="wb_plane", align_bytes=64)
        xa_words = sb.tile([P, J], U16, name="xa_words", align_bytes=64)
        xa_plane = sb.tile([P, J], U8, name="xa_plane", align_bytes=64)
        xb_words = sb.tile([P, I], U16, name="xb_words", align_bytes=64)
        xb_plane = sb.tile([P, I], U8, name="xb_plane", align_bytes=64)
        lagged = sb.tile([P, PACK * (I + 1)], F32, name="lagged", align_bytes=64)
        before = [sb.tile([P, I + 4], F32, name=f"before{a}", align_bytes=64) for a in range(2)]

        nc.gpsimd.memset(wa_plane_in[:].bitcast(I32), 0)
        nc.gpsimd.memset(wb_plane_in[:].bitcast(I32), 0)
        nc.gpsimd.memset(lagged[:, 0:PACK], 0.0)
        for a in range(2):
            nc.gpsimd.memset(before[a][:, 3:4], 0.0)

        nc.sync.dma_start(list_a[:], offs)
        nc.scalar.dma_start(out=x_words[:].bitcast(I32), in_=xt_words[0].bitcast(I32))
        load_scale_rows_repeated([nc.sync, nc.scalar, nc.sync, nc.scalar], x_plane, xt_scales)
        nc.sync.dma_start(list_b[:], offs2)
        nc.sync.dma_start(out=wa_in[:].bitcast(I32), in_=wa_words[0].bitcast(I32))
        load_scale_rows([nc.sync] * 4, wa_plane_in, wa_scales)
        nc.sync.dma_start(out=wb_in[:].bitcast(I32), in_=wb_words[0].rearrange("p n t -> p (n t)").bitcast(I32))
        load_scale_rows([nc.gpsimd] + [nc.sync] * 3, wb_plane_in, wb_scales)

        nc.vector.tensor_copy(xa_words[:], x_words[:].indirect(list_a[:]))
        nc.vector.tensor_copy(xa_plane[:], x_plane[:].indirect(list_a[:]))
        nc.vector.tensor_copy(xb_words[:], x_words[:].indirect(list_b[:]))
        nc.vector.tensor_copy(xb_plane[:], x_plane[:].indirect(list_b[:]))

        deal_columns(nc, wa, wa_in)
        deal_columns(nc, wa_plane, wa_plane_in)
        deal_columns(nc, wb, wb_in)
        deal_columns(nc, wb_plane, wb_plane_in)

        za = [ps.tile([P, PACK, HALF], F32, name=f"za{h}") for h in range(2)]
        zb = [ps.tile([P, PACK, HALF], F32, name=f"zb{h}") for h in range(2)]
        scores = [[ps.tile([P, HALF], F32, name=f"scores{h}{a}") for a in range(2)] for h in range(2)]

        for h in range(2):
            cols = slice(h * HALF, (h + 1) * HALF)
            for t in range(PACK):
                nc.tensor.matmul_mx(
                    out=za[h][:, t, :],
                    lhsT=wa[:, 2 * P * t : 2 * P * (t + 1)].bitcast(E2M1),
                    lhsT_scale=wa_plane[:, P * t : P * (t + 1)],
                    rhs=xa_words[:, cols].bitcast(E2M1),
                    rhs_scale=xa_plane[:, cols],
                    start=True,
                    stop=True,
                )
        for h in range(2):
            cols = slice(h * HALF, (h + 1) * HALF)
            for t in range(PACK):
                nc.tensor.matmul_mx(
                    out=zb[h][:, t, :],
                    lhsT=wb[:, 4 * P * t : 4 * P * (t + 1)].bitcast(E5M2),
                    lhsT_scale=wb_plane[:, P * t : P * (t + 1)],
                    rhs=xb_words[:, cols].bitcast(E2M1),
                    rhs_scale=xb_plane[:, cols],
                    start=True,
                    stop=True,
                )

        bundles = HALF // BUNDLE
        sums = [sb.tile([P, bundles, PACK], F32, name=f"sums{h}", align_bytes=64) for h in range(2)]
        means = [sb.tile([P, bundles, PACK], F32, name=f"means{h}", align_bytes=64) for h in range(2)]
        ha = sb.tile([P, J * PACK], BF16, name="ha", align_bytes=64)
        ha_codes = sb.tile([P, J], U32, name="ha_codes", align_bytes=64)
        ha_plane = sb.tile([P, J], U8, name="ha_plane", align_bytes=64)
        for h in range(2):
            nc.vector.tensor_reduce(
                out=sums[h][:],
                in_=za[h][:].rearrange("p t (e u) -> p e t u", u=BUNDLE),
                axis=mybir.AxisListType.X,
                op=ALU.add,
            )
            nc.gpsimd.tensor_scalar(
                out=means[h][:],
                in0=sums[h][:],
                scalar1=1.0 / BUNDLE,
                scalar2=0.0,
                op0=ALU.mult,
                op1=ALU.add,
            )
        for h in range(2):
            nc.vector.tensor_tensor(
                out=ha[:, h * HALF * PACK : (h + 1) * HALF * PACK].rearrange("p (e u t) -> p e u t", u=BUNDLE, t=PACK),
                in0=za[h][:].rearrange("p t (e u) -> p e u t", u=BUNDLE),
                in1=means[h][:].unsqueeze(2).broadcast_to([P, bundles, BUNDLE, PACK]),
                op=ALU.subtract,
            )

        hb = [sb.tile([P, HALF * PACK], BF16, name=f"hb{h}", align_bytes=64) for h in range(2)]
        hb_codes = [sb.tile([P, HALF], U32, name=f"hb_codes{h}", align_bytes=64) for h in range(2)]
        hb_plane = [sb.tile([P, HALF], U8, name=f"hb_plane{h}", align_bytes=64) for h in range(2)]
        steps = [sb.tile([P, 2, HALF], F32, name=f"steps{h}", align_bytes=64) for h in range(2)]
        result = [[sb.tile([P, HALF], F32, name=f"result{h}{a}", align_bytes=64) for a in range(2)] for h in range(2)]

        def lag(h):
            start = PACK * (h * HALF + 1)
            nc.scalar.activation(
                out=lagged[:, start : start + PACK * HALF].rearrange("p (i t) -> p i t", t=PACK),
                in_=zb[h][:].rearrange("p t i -> p i t"),
                func=ACT.Copy,
                scale=-LAG,
            )

        def make_hb(h):
            start = PACK * h * HALF
            nc.vector.tensor_tensor(
                out=hb[h][:].rearrange("p (i t) -> p i t", t=PACK),
                in0=zb[h][:].rearrange("p t i -> p i t"),
                in1=lagged[:, start : start + PACK * HALF].rearrange("p (i t) -> p i t", t=PACK),
                op=ALU.add,
            )

        def quantize_hb(h):
            nc.vector.quantize_mx(out=hb_codes[h][:].bitcast(E4M3), scales=hb_plane[h][:], in_=hb[h][:])

        def meet(h):
            for a in range(2):
                rows = slice(a * P, (a + 1) * P)
                nc.tensor.matmul_mx(
                    out=scores[h][a][:],
                    lhsT=ha_codes[:, rows].bitcast(E5M2),
                    lhsT_scale=ha_plane[:, rows],
                    rhs=hb_codes[h][:].bitcast(E4M3),
                    rhs_scale=hb_plane[h][:],
                    start=True,
                    stop=True,
                )
            for a in range(2):
                nc.scalar.copy(out=before[a][:, 4 + h * HALF : 4 + (h + 1) * HALF], in_=scores[h][a][:])

        def finish(h):
            for a in range(2):
                nc.vector.tensor_tensor(
                    out=steps[h][:, a, :],
                    in0=scores[h][a][:],
                    in1=before[a][:, 3 + h * HALF : 3 + (h + 1) * HALF],
                    op=ALU.subtract,
                )
            for a, queue in enumerate((nc.sync, nc.scalar)):
                nc.scalar.activation(out=result[h][a][:], in_=steps[h][:, a, :], func=ACT.Abs, scale=GAIN)
                queue.dma_start(out=out[a * P : (a + 1) * P, h * HALF : (h + 1) * HALF], in_=result[h][a][:])

        lag(0)
        lag(1)
        make_hb(0)
        nc.vector.quantize_mx(out=ha_codes[:].bitcast(E5M2), scales=ha_plane[:], in_=ha[:])
        quantize_hb(0)
        make_hb(1)
        meet(0)
        quantize_hb(1)
        meet(1)
        finish(0)
        finish(1)
